import numpy as np
import ml_dtypes


def mxq(x, axis, fmt="e4m3"):
    dtype, down = {"e4m3": (ml_dtypes.float8_e4m3fn, 7), "e5m2": (ml_dtypes.float8_e5m2, 14)}[fmt]
    v = np.moveaxis(np.asarray(x, np.float32).astype(ml_dtypes.bfloat16).astype(np.float64), axis, -1)
    blocks = v.reshape(v.shape[:-1] + (-1, 32))
    amax = np.abs(blocks).max(-1, keepdims=True)
    byte = np.maximum(np.where(amax > 0, np.frexp(amax)[1] - 1 + 127, 0) - down, 1)
    scale = np.exp2(byte - 127.0)
    codes = (blocks / scale).astype(np.float32).astype(dtype).astype(np.float64)
    return np.moveaxis((codes * scale).reshape(v.shape), -1, axis)


WIDE = False


def mx_kscale(k):
    if not WIDE:
        return np.ones(k)
    levels = np.array([10, -10, 5, -5, 0])
    if k % 512:
        return np.exp2(np.random.permutation(np.resize(levels, k // 32))).repeat(32)
    a = np.empty((k // 512, 16))
    for p in range(k // 512):
        a[p, :8] = np.random.permutation(np.resize(levels, 8))
        for g in range(8):
            far = levels[np.abs(levels - a[p, g]) >= 10]
            a[p, g + 8] = far[np.random.randint(len(far))]
    return np.exp2(a.ravel()).repeat(32)


def f64(x):
    return np.asarray(x).astype(np.float64)


def striped8(idx):
    return np.concatenate([x.reshape(-1, 16).T for x in idx]).astype(np.uint16)


def runs(offs, k):
    lists = np.stack([offs[16 * r : 16 * r + 16].T.reshape(-1) for r in range(8)]).astype(np.int64)
    return lists[np.arange(k) % 512 // 64]


def pack_weight(w):
    k, n = w.shape
    w = f64(np.asarray(w, np.float32).astype(ml_dtypes.bfloat16)).reshape(k // 32, 32, n)
    amax = np.abs(w).max(1)
    byte = np.clip(np.where(amax > 0, np.frexp(amax)[1] - 1 + 127 - 7, 1), 1, 254)
    scaled = (w * np.exp2(127.0 - byte)[:, None, :]).reshape(k, n).astype(np.float32)
    words = np.ascontiguousarray(scaled.reshape(k // 512, 128, 4, n).transpose(0, 1, 3, 2)).astype(ml_dtypes.float8_e4m3fn).view(np.uint8)
    return words, np.ascontiguousarray(byte.astype(np.uint8).reshape(k // 512, 16, n))


def unpack_weight(words, scales):
    g, p, n, _ = words.shape
    vals = np.ascontiguousarray(words).view(ml_dtypes.float8_e4m3fn).astype(np.float64) * np.repeat(np.exp2(scales.astype(np.float64) - 127.0), 8, axis=1)[..., None]
    return vals.transpose(0, 1, 3, 2).reshape(g * 512, n)


def relu(v):
    return np.maximum(v, 0.0)


K, T, S, H, N = 1024, 2048, 512, 512, 128


def setup_inputs():
    n = np.random.standard_normal
    s = mx_kscale(K)[:, None]
    u = mx_kscale(H)
    packed_xT = pack_weight(n((K, T)) * s)
    packed_w2 = pack_weight(n((H, N)) / np.sqrt(H) / u[:, None])
    return {
        "x_words": packed_xT[0],
        "x_scales": packed_xT[1],
        "w1": (n((K, H)) / np.sqrt(K) / s * u).astype(np.float32),
        "w2_words": packed_w2[0],
        "w2_scales": packed_w2[1],
        "offs": striped8(np.stack([np.random.permutation(T)[:S] for _ in range(8)])),
    }


def reference(x_words, x_scales, w1, w2_words, w2_scales, offs):
    xq = unpack_weight(x_words, x_scales)[np.arange(K)[:, None], runs(offs, K)]
    h = relu(mxq(f64(w1), 0, "e4m3").T @ xq)
    return unpack_weight(w2_words, w2_scales).T @ mxq(h, 0, "e4m3")

@@ -1,0 +1,133 @@
+from contextlib import ExitStack
+
+import concourse.mybir as mybir
+
+K, T, S, H, N = 1024, 2048, 512, 512, 128
+FLOPS = 2 * K * H * S + 2 * H * N * S
+
+F32 = mybir.dt.float32
+BF16 = mybir.dt.bfloat16
+I32 = mybir.dt.int32
+U32 = mybir.dt.uint32
+U16 = mybir.dt.uint16
+U8 = mybir.dt.uint8
+FP8X4 = mybir.dt.float8_e4m3fn_x4
+COPY = mybir.ActivationFunctionType.Copy
+RELU = mybir.ActivationFunctionType.Relu
+
+P = 128
+PACK = 4
+PASSES = K // (P * PACK)
+HALF = S // 2
+QUARTER = S // 4
+PLANE_STEP = 8
+M_VECTOR = 80
+
+
+def tile_picked_phmlp_relu_p_kernel(
+    tc, x_words, x_scales, w1, w2_words, w2_scales, offs, out
+):
+    nc = tc.nc
+    with ExitStack() as ctx:
+        keep = ctx.enter_context(tc.tile_pool(name="keep", bufs=1))
+        psum = ctx.enter_context(tc.psum_pool(name="psum", bufs=1))
+
+        offsets = keep.tile([P, S // 16], U16, name="offsets")
+        nc.sync.dma_start(offsets[:], offs)
+
+        scale_table = keep.tile([P, T], U8, name="scale_table", align_bytes=64)
+        nc.vector.memset(scale_table[:].bitcast(I32), 0)
+        scale_rows = x_scales.bitcast(I32).rearrange("z (r e) c -> e r z c", e=2)
+        for e in range(2):
+            nc.scalar.dma_start(scale_table[e:P:PLANE_STEP, :].bitcast(I32), scale_rows[e])
+
+        w1_raw = []
+        for z in range(PASSES):
+            raw = keep.tile([P, PACK, H], F32, name=f"w1_raw{z}")
+            nc.sync.dma_start(raw[:], w1[z * 512 : (z + 1) * 512, :].rearrange("(p j) c -> p j c", j=PACK))
+            w1_raw.append(raw)
+        word_table = []
+        for z in range(PASSES):
+            table = keep.tile([P, T], I32, name=f"word_table{z}", align_bytes=64)
+            nc.sync.dma_start(table[:], x_words[z].rearrange("p n t -> p (n t)").bitcast(I32))
+            word_table.append(table)
+
+        w2_codes = keep.tile([P, N], I32, name="w2_codes", align_bytes=64)
+        w2_plane = keep.tile([P, N], U8, name="w2_plane", align_bytes=64)
+        nc.gpsimd.memset(w2_plane[:], 0)
+        nc.gpsimd.dma_start(w2_codes[:], w2_words[0].rearrange("p n t -> p (n t)").bitcast(I32))
+        for q in range(4):
+            nc.gpsimd.dma_start(
+                w2_plane[32 * q : 32 * q + 4, :].bitcast(I32), w2_scales[0, 4 * q : 4 * q + 4, :].bitcast(I32)
+            )
+
+        picked_scales = keep.tile([P, S], U8, name="picked_scales", align_bytes=64)
+        nc.vector.tensor_copy(picked_scales[:], scale_table[:].indirect(offsets[:]))
+        x_plane = keep.tile([P, S], U8, name="x_plane", align_bytes=64)
+        nc.vector.tensor_copy(x_plane[:].bitcast(I32), picked_scales[:].bitcast(I32))
+        for z in range(PASSES):
+            for e in range(2):
+                row = PLANE_STEP * z + e
+                nc.scalar.dma_start(
+                    x_plane[row + 2 : P : 32, :].bitcast(I32), picked_scales[row + 16 : P : 32, :].bitcast(I32)
+                )
+
+        w1_codes, w1_plane = [], []
+        for z in range(PASSES):
+            grouped = keep.tile([P, PACK, P, PACK], BF16, name=f"w1_grouped{z}", align_bytes=64)
+            dst = grouped[:].rearrange("p t m j -> p m j t")
+            src = w1_raw[z][:].rearrange("p j (m t) -> p m j t", t=PACK)
+            nc.vector.tensor_copy(dst[:, :M_VECTOR], src[:, :M_VECTOR])
+            nc.scalar.activation(dst[:, M_VECTOR:], src[:, M_VECTOR:], COPY)
+            codes = keep.tile([P, H], U32, name=f"w1_codes{z}", align_bytes=64)
+            plane = keep.tile([P, H], U8, name=f"w1_plane{z}", align_bytes=64)
+            nc.vector.quantize_mx(
+                out=codes[:].bitcast(FP8X4), scales=plane[:], in_=grouped[:].rearrange("p t m j -> p (t m j)")
+            )
+            w1_codes.append(codes)
+            w1_plane.append(plane)
+
+        hidden = [psum.tile([P, PACK, QUARTER], F32, name=f"hidden{u}") for u in range(4)]
+        for z in range(PASSES):
+            for half in range(2):
+                picked = keep.tile([P, HALF], U32, name=f"picked{z}_{half}", align_bytes=64)
+                cols = slice(half * HALF // 16, (half + 1) * HALF // 16)
+                nc.vector.tensor_copy(picked[:], word_table[z][:].bitcast(U32).indirect(offsets[:, cols]))
+                for v in range(2):
+                    u = 2 * half + v
+                    for t in range(PACK):
+                        nc.tensor.matmul_mx(
+                            out=hidden[u][:, t, :],
+                            lhsT=w1_codes[z][:, t * P : (t + 1) * P].bitcast(FP8X4),
+                            lhsT_scale=w1_plane[z][:, t * P : (t + 1) * P],
+                            rhs=picked[:, v * QUARTER : (v + 1) * QUARTER].bitcast(FP8X4),
+                            rhs_scale=x_plane[PLANE_STEP * z :, u * QUARTER : (u + 1) * QUARTER],
+                            start=(z == 0 and t == 0),
+                            stop=(z == PASSES - 1 and t == PACK - 1),
+                        )
+
+        for u in range(4):
+            h = keep.tile([P, QUARTER, PACK], BF16, name=f"h{u}", align_bytes=64)
+            sums = hidden[u][:].rearrange("p t n -> p n t")
+            if u % 2 == 0:
+                nc.scalar.activation(h[:], sums, RELU)
+            else:
+                nc.vector.tensor_scalar_max(h[:], sums, 0.0)
+            h_codes = keep.tile([P, QUARTER], U32, name=f"h_codes{u}", align_bytes=64)
+            h_plane = keep.tile([P, QUARTER], U8, name=f"h_plane{u}", align_bytes=64)
+            nc.vector.quantize_mx(
+                out=h_codes[:].bitcast(FP8X4), scales=h_plane[:], in_=h[:].rearrange("p n t -> p (n t)")
+            )
+            acc = psum.tile([P, QUARTER], F32, name=f"acc{u}")
+            nc.tensor.matmul_mx(
+                out=acc[:],
+                lhsT=w2_codes[:].bitcast(FP8X4),
+                lhsT_scale=w2_plane[:],
+                rhs=h_codes[:].bitcast(FP8X4),
+                rhs_scale=h_plane[:],
+                start=True,
+                stop=True,
+            )
+            result = keep.tile([P, QUARTER], F32, name=f"result{u}")
+            nc.scalar.copy(result[:], acc[:])
+            nc.sync.dma_start(out[:, u * QUARTER : (u + 1) * QUARTER], result[:])

@@ -32,20 +32,25 @@ def tile_picked_phmlp_relu_p_kernel(
         keep = ctx.enter_context(tc.tile_pool(name="keep", bufs=1))
         psum = ctx.enter_context(tc.psum_pool(name="psum", bufs=1))
 
+        warm = keep.tile([P, 2], F32, name="warm")
+        nc.gpsimd.memset(warm[:, 0:1], 0.0)
+        nc.scalar.activation(warm[:, 1:2], warm[:, 0:1], RELU)
+
         offsets = keep.tile([P, S // 16], U16, name="offsets")
         nc.sync.dma_start(offsets[:], offs)
 
         scale_table = keep.tile([P, T], U8, name="scale_table", align_bytes=64)
         nc.vector.memset(scale_table[:].bitcast(I32), 0)
         scale_rows = x_scales.bitcast(I32).rearrange("z (r e) c -> e r z c", e=2)
-        for e in range(2):
-            nc.scalar.dma_start(scale_table[e:P:PLANE_STEP, :].bitcast(I32), scale_rows[e])
 
         w1_raw = []
         for z in range(PASSES):
             raw = keep.tile([P, PACK, H], F32, name=f"w1_raw{z}")
             nc.sync.dma_start(raw[:], w1[z * 512 : (z + 1) * 512, :].rearrange("(p j) c -> p j c", j=PACK))
             w1_raw.append(raw)
+            if z == 0:
+                for e in range(2):
+                    nc.sync.dma_start(scale_table[e:P:PLANE_STEP, :].bitcast(I32), scale_rows[e])
         word_table = []
         for z in range(PASSES):
             table = keep.tile([P, T], I32, name=f"word_table{z}", align_bytes=64)
@@ -75,8 +80,8 @@ def tile_picked_phmlp_relu_p_kernel(
         w1_codes, w1_plane = [], []
         for z in range(PASSES):
             grouped = keep.tile([P, PACK, P, PACK], BF16, name=f"w1_grouped{z}", align_bytes=64)
-            dst = grouped[:].rearrange("p t m j -> p m j t")
-            src = w1_raw[z][:].rearrange("p j (m t) -> p m j t", t=PACK)
+            dst = grouped[:].rearrange("p t m j -> p m t j")
+            src = w1_raw[z][:].rearrange("p j (m t) -> p m t j", t=PACK)
             nc.vector.tensor_copy(dst[:, :M_VECTOR], src[:, :M_VECTOR])
             nc.scalar.activation(dst[:, M_VECTOR:], src[:, M_VECTOR:], COPY)
             codes = keep.tile([P, H], U32, name=f"w1_codes{z}", align_bytes=64)

@@ -45,17 +45,23 @@ def tile_picked_phmlp_relu_p_kernel(
 
         w1_raw = []
         for z in range(PASSES):
-            raw = keep.tile([P, PACK, H], F32, name=f"w1_raw{z}")
-            nc.sync.dma_start(raw[:], w1[z * 512 : (z + 1) * 512, :].rearrange("(p j) c -> p j c", j=PACK))
-            w1_raw.append(raw)
+            raw = keep.tile([P, PACK, H], F32, name=f"w1_raw{z}", tag=f"big{z}", align_bytes=64)
+            rows = w1[z * 512 : (z + 1) * 512, :].rearrange("(p j) c -> p j c", j=PACK)
             if z == 0:
+                nc.sync.dma_start(raw[:, :2, :], rows[:, :2, :])
                 for e in range(2):
                     nc.sync.dma_start(scale_table[e:P:PLANE_STEP, :].bitcast(I32), scale_rows[e])
-        word_table = []
-        for z in range(PASSES):
-            table = keep.tile([P, T], I32, name=f"word_table{z}", align_bytes=64)
+                nc.sync.dma_start(raw[:, 2:, :], rows[:, 2:, :])
+            else:
+                nc.sync.dma_start(raw[:], rows)
+            w1_raw.append(raw)
+
+        def load_words(z, tag):
+            table = keep.tile([P, T], I32, name=f"word_table{z}", tag=tag, align_bytes=64)
             nc.sync.dma_start(table[:], x_words[z].rearrange("p n t -> p (n t)").bitcast(I32))
-            word_table.append(table)
+            return table
+
+        word_table = [load_words(0, "big2")]
 
         w2_codes = keep.tile([P, N], I32, name="w2_codes", align_bytes=64)
         w2_plane = keep.tile([P, N], U8, name="w2_plane", align_bytes=64)
@@ -73,7 +79,7 @@ def tile_picked_phmlp_relu_p_kernel(
         for z in range(PASSES):
             for e in range(2):
                 row = PLANE_STEP * z + e
-                nc.scalar.dma_start(
+                nc.sync.dma_start(
                     x_plane[row + 2 : P : 32, :].bitcast(I32), picked_scales[row + 16 : P : 32, :].bitcast(I32)
                 )
 
@@ -91,6 +97,8 @@ def tile_picked_phmlp_relu_p_kernel(
             )
             w1_codes.append(codes)
             w1_plane.append(plane)
+            if z == 0:
+                word_table.append(load_words(1, "big0"))
 
         hidden = [psum.tile([P, PACK, QUARTER], F32, name=f"hidden{u}") for u in range(4)]
         for z in range(PASSES):

@@ -17,7 +17,10 @@ RELU = mybir.ActivationFunctionType.Relu
 
 P = 128
 PACK = 4
-PASSES = K // (P * PACK)
+K_PASS = P * PACK
+PASSES = K // K_PASS
+QUADRANT = 32
+GROUP = 16
 HALF = S // 2
 QUARTER = S // 4
 PLANE_STEP = 8
@@ -32,47 +35,29 @@ def tile_picked_phmlp_relu_p_kernel(
         keep = ctx.enter_context(tc.tile_pool(name="keep", bufs=1))
         psum = ctx.enter_context(tc.psum_pool(name="psum", bufs=1))
 
-        warm = keep.tile([P, 2], F32, name="warm")
-        nc.gpsimd.memset(warm[:, 0:1], 0.0)
-        nc.scalar.activation(warm[:, 1:2], warm[:, 0:1], RELU)
-
-        offsets = keep.tile([P, S // 16], U16, name="offsets")
-        nc.sync.dma_start(offsets[:], offs)
-
-        scale_table = keep.tile([P, T], U8, name="scale_table", align_bytes=64)
-        nc.vector.memset(scale_table[:].bitcast(I32), 0)
-        scale_rows = x_scales.bitcast(I32).rearrange("z (r e) c -> e r z c", e=2)
-
-        w1_raw = []
-        for z in range(PASSES):
-            raw = keep.tile([P, PACK, H], F32, name=f"w1_raw{z}", tag=f"big{z}", align_bytes=64)
-            rows = w1[z * 512 : (z + 1) * 512, :].rearrange("(p j) c -> p j c", j=PACK)
-            if z == 0:
-                nc.sync.dma_start(raw[:, :2, :], rows[:, :2, :])
-                for e in range(2):
-                    nc.sync.dma_start(scale_table[e:P:PLANE_STEP, :].bitcast(I32), scale_rows[e])
-                nc.sync.dma_start(raw[:, 2:, :], rows[:, 2:, :])
-            else:
-                nc.sync.dma_start(raw[:], rows)
-            w1_raw.append(raw)
+        def w1_rows(z):
+            return w1[z * K_PASS : (z + 1) * K_PASS, :].rearrange("(p j) c -> p j c", j=PACK)
 
         def load_words(z, tag):
-            table = keep.tile([P, T], I32, name=f"word_table{z}", tag=tag, align_bytes=64)
-            nc.sync.dma_start(table[:], x_words[z].rearrange("p n t -> p (n t)").bitcast(I32))
+            table = keep.tile([P, T], I32, name=f"word_table{z}", tag=tag, align_bytes=256)
+            nc.sync.dma_start(table[:], x_words[z].rearrange("p c j -> p (c j)").bitcast(I32))
             return table
 
-        word_table = [load_words(0, "big2")]
+        offsets = keep.tile([P, S // GROUP], U16, name="offsets")
+        nc.sync.dma_start(offsets[:], offs)
 
-        w2_codes = keep.tile([P, N], I32, name="w2_codes", align_bytes=64)
-        w2_plane = keep.tile([P, N], U8, name="w2_plane", align_bytes=64)
-        nc.gpsimd.memset(w2_plane[:], 0)
-        nc.gpsimd.dma_start(w2_codes[:], w2_words[0].rearrange("p n t -> p (n t)").bitcast(I32))
-        for q in range(4):
-            nc.gpsimd.dma_start(
-                w2_plane[32 * q : 32 * q + 4, :].bitcast(I32), w2_scales[0, 4 * q : 4 * q + 4, :].bitcast(I32)
-            )
+        scale_table = keep.tile([P, T], U8, name="scale_table", align_bytes=256)
+        nc.vector.memset(scale_table[:].bitcast(I32), 0)
+        scale_rows = x_scales.bitcast(I32).rearrange("z (g e) c -> e g z c", e=2)
+        w1_raw = [keep.tile([P, PACK, H], F32, name=f"w1_raw{z}", align_bytes=256) for z in range(PASSES)]
+        nc.sync.dma_start(w1_raw[0][:, :2, :], w1_rows(0)[:, :2, :])
+        for e in range(2):
+            nc.sync.dma_start(scale_table[e:P:PLANE_STEP, :].bitcast(I32), scale_rows[e])
+        nc.sync.dma_start(w1_raw[0][:, 2:, :], w1_rows(0)[:, 2:, :])
+        word_table = [load_words(0, "word_table0")]
+        nc.sync.dma_start(w1_raw[1][:], w1_rows(1))
 
-        picked_scales = keep.tile([P, S], U8, name="picked_scales", align_bytes=64)
+        picked_scales = keep.tile([P, S], U8, name="picked_scales", align_bytes=256)
         nc.vector.tensor_copy(picked_scales[:], scale_table[:].indirect(offsets[:]))
         x_plane = keep.tile([P, S], U8, name="x_plane", align_bytes=64)
         nc.vector.tensor_copy(x_plane[:].bitcast(I32), picked_scales[:].bitcast(I32))
@@ -80,58 +65,64 @@ def tile_picked_phmlp_relu_p_kernel(
             for e in range(2):
                 row = PLANE_STEP * z + e
                 nc.sync.dma_start(
-                    x_plane[row + 2 : P : 32, :].bitcast(I32), picked_scales[row + 16 : P : 32, :].bitcast(I32)
+                    x_plane[row + 2 : P : QUADRANT, :].bitcast(I32),
+                    x_plane[row + GROUP : P : QUADRANT, :].bitcast(I32),
                 )
+        word_table.append(load_words(1, "picked_scales"))
 
-        w1_codes, w1_plane = [], []
+        hidden = [psum.tile([P, PACK, QUARTER], F32, name=f"hidden{u}") for u in range(S // QUARTER)]
         for z in range(PASSES):
             grouped = keep.tile([P, PACK, P, PACK], BF16, name=f"w1_grouped{z}", align_bytes=64)
-            dst = grouped[:].rearrange("p t m j -> p m t j")
-            src = w1_raw[z][:].rearrange("p j (m t) -> p m t j", t=PACK)
-            nc.vector.tensor_copy(dst[:, :M_VECTOR], src[:, :M_VECTOR])
-            nc.scalar.activation(dst[:, M_VECTOR:], src[:, M_VECTOR:], COPY)
-            codes = keep.tile([P, H], U32, name=f"w1_codes{z}", align_bytes=64)
-            plane = keep.tile([P, H], U8, name=f"w1_plane{z}", align_bytes=64)
+            rounded = grouped[:].rearrange("p t m j -> p m t j")
+            exact = w1_raw[z][:].rearrange("p j (m t) -> p m t j", t=PACK)
+            nc.vector.tensor_copy(rounded[:, :M_VECTOR], exact[:, :M_VECTOR])
+            nc.scalar.activation(rounded[:, M_VECTOR:], exact[:, M_VECTOR:], COPY)
+            w1_codes = keep.tile([P, H], U32, name=f"w1_codes{z}", align_bytes=64)
+            w1_plane = keep.tile([P, H], U8, name=f"w1_plane{z}", align_bytes=64)
             nc.vector.quantize_mx(
-                out=codes[:].bitcast(FP8X4), scales=plane[:], in_=grouped[:].rearrange("p t m j -> p (t m j)")
+                out=w1_codes[:].bitcast(FP8X4), scales=w1_plane[:], in_=grouped[:].rearrange("p t m j -> p (t m j)")
             )
-            w1_codes.append(codes)
-            w1_plane.append(plane)
-            if z == 0:
-                word_table.append(load_words(1, "big0"))
 
-        hidden = [psum.tile([P, PACK, QUARTER], F32, name=f"hidden{u}") for u in range(4)]
-        for z in range(PASSES):
-            for half in range(2):
+            for half in range(S // HALF):
                 picked = keep.tile([P, HALF], U32, name=f"picked{z}_{half}", align_bytes=64)
-                cols = slice(half * HALF // 16, (half + 1) * HALF // 16)
-                nc.vector.tensor_copy(picked[:], word_table[z][:].bitcast(U32).indirect(offsets[:, cols]))
-                for v in range(2):
-                    u = 2 * half + v
+                entries = offsets[:, half * HALF // GROUP : (half + 1) * HALF // GROUP]
+                nc.vector.tensor_copy(picked[:], word_table[z][:].bitcast(U32).indirect(entries))
+                for v in range(HALF // QUARTER):
+                    u = half * HALF // QUARTER + v
                     for t in range(PACK):
                         nc.tensor.matmul_mx(
                             out=hidden[u][:, t, :],
-                            lhsT=w1_codes[z][:, t * P : (t + 1) * P].bitcast(FP8X4),
-                            lhsT_scale=w1_plane[z][:, t * P : (t + 1) * P],
+                            lhsT=w1_codes[:, t * P : (t + 1) * P].bitcast(FP8X4),
+                            lhsT_scale=w1_plane[:, t * P : (t + 1) * P],
                             rhs=picked[:, v * QUARTER : (v + 1) * QUARTER].bitcast(FP8X4),
                             rhs_scale=x_plane[PLANE_STEP * z :, u * QUARTER : (u + 1) * QUARTER],
                             start=(z == 0 and t == 0),
                             stop=(z == PASSES - 1 and t == PACK - 1),
                         )
 
-        for u in range(4):
+        w2_codes = keep.tile([P, N], I32, name="w2_codes", tag="w1_raw1", align_bytes=256)
+        nc.sync.dma_start(w2_codes[:], w2_words[0].rearrange("p c j -> p (c j)").bitcast(I32))
+        w2_plane = keep.tile([P, N], U8, name="w2_plane", tag="w1_raw0", align_bytes=256)
+        nc.gpsimd.memset(w2_plane[:].bitcast(I32), 0)
+        for q in range(P // QUADRANT):
+            nc.sync.dma_start(
+                w2_plane[QUADRANT * q : QUADRANT * q + 4, :].bitcast(I32),
+                w2_scales[0, 4 * q : 4 * q + 4, :].bitcast(I32),
+            )
+
+        for u in range(S // QUARTER):
             h = keep.tile([P, QUARTER, PACK], BF16, name=f"h{u}", align_bytes=64)
             sums = hidden[u][:].rearrange("p t n -> p n t")
             if u % 2 == 0:
-                nc.scalar.activation(h[:], sums, RELU)
-            else:
                 nc.vector.tensor_scalar_max(h[:], sums, 0.0)
+            else:
+                nc.scalar.activation(h[:], sums, RELU)
             h_codes = keep.tile([P, QUARTER], U32, name=f"h_codes{u}", align_bytes=64)
             h_plane = keep.tile([P, QUARTER], U8, name=f"h_plane{u}", align_bytes=64)
             nc.vector.quantize_mx(
                 out=h_codes[:].bitcast(FP8X4), scales=h_plane[:], in_=h[:].rearrange("p n t -> p (n t)")
             )
-            acc = psum.tile([P, QUARTER], F32, name=f"acc{u}")
+            acc = psum.tile([N, QUARTER], F32, name=f"acc{u}")
             nc.tensor.matmul_mx(
                 out=acc[:],
                 lhsT=w2_codes[:].bitcast(FP8X4),
@@ -141,6 +132,6 @@ def tile_picked_phmlp_relu_p_kernel(
                 start=True,
                 stop=True,
             )
-            result = keep.tile([P, QUARTER], F32, name=f"result{u}")
+            result = keep.tile([N, QUARTER], F32, name=f"result{u}")
             nc.scalar.copy(result[:], acc[:])
             nc.sync.dma_start(out[:, u * QUARTER : (u + 1) * QUARTER], result[:])

@@ -24,7 +24,7 @@ GROUP = 16
 HALF = S // 2
 QUARTER = S // 4
 PLANE_STEP = 8
-M_VECTOR = 80
+M_VECTOR = 88
 
 
 def tile_picked_phmlp_relu_p_kernel(
@@ -44,13 +44,13 @@ def tile_picked_phmlp_relu_p_kernel(
             return table
 
         offsets = keep.tile([P, S // GROUP], U16, name="offsets")
-        nc.sync.dma_start(offsets[:], offs)
 
         scale_table = keep.tile([P, T], U8, name="scale_table", align_bytes=256)
         nc.vector.memset(scale_table[:].bitcast(I32), 0)
         scale_rows = x_scales.bitcast(I32).rearrange("z (g e) c -> e g z c", e=2)
         w1_raw = [keep.tile([P, PACK, H], F32, name=f"w1_raw{z}", align_bytes=256) for z in range(PASSES)]
         nc.sync.dma_start(w1_raw[0][:, :2, :], w1_rows(0)[:, :2, :])
+        nc.sync.dma_start(offsets[:], offs)
         for e in range(2):
             nc.sync.dma_start(scale_table[e:P:PLANE_STEP, :].bitcast(I32), scale_rows[e])
         nc.sync.dma_start(w1_raw[0][:, 2:, :], w1_rows(0)[:, 2:, :])
@@ -110,19 +110,24 @@ def tile_picked_phmlp_relu_p_kernel(
                 w2_scales[0, 4 * q : 4 * q + 4, :].bitcast(I32),
             )
 
-        for u in range(S // QUARTER):
-            h = keep.tile([P, QUARTER, PACK], BF16, name=f"h{u}", align_bytes=64)
-            sums = hidden[u][:].rearrange("p t n -> p n t")
-            if u % 2 == 0:
-                nc.vector.tensor_scalar_max(h[:], sums, 0.0)
-            else:
-                nc.scalar.activation(h[:], sums, RELU)
-            h_codes = keep.tile([P, QUARTER], U32, name=f"h_codes{u}", align_bytes=64)
-            h_plane = keep.tile([P, QUARTER], U8, name=f"h_plane{u}", align_bytes=64)
+        def relu_rounded(banks):
+            h = keep.tile([P, len(banks), QUARTER, PACK], BF16, name=f"h{banks[0]}", align_bytes=64)
+            for slot, u in enumerate(banks):
+                sums = hidden[u][:].rearrange("p t n -> p n t")
+                if u % 2 == 0:
+                    nc.vector.tensor_scalar_max(h[:, slot], sums, 0.0)
+                else:
+                    nc.scalar.activation(h[:, slot], sums, RELU)
+            return h
+
+        def second_product(banks, h, copy_out):
+            width = len(banks) * QUARTER
+            h_codes = keep.tile([P, width], U32, name=f"h_codes{banks[0]}", align_bytes=64)
+            h_plane = keep.tile([P, width], U8, name=f"h_plane{banks[0]}", align_bytes=64)
             nc.vector.quantize_mx(
-                out=h_codes[:].bitcast(FP8X4), scales=h_plane[:], in_=h[:].rearrange("p n t -> p (n t)")
+                out=h_codes[:].bitcast(FP8X4), scales=h_plane[:], in_=h[:].rearrange("p s n t -> p (s n t)")
             )
-            acc = psum.tile([N, QUARTER], F32, name=f"acc{u}")
+            acc = psum.tile([N, width], F32, name=f"acc{banks[0]}")
             nc.tensor.matmul_mx(
                 out=acc[:],
                 lhsT=w2_codes[:].bitcast(FP8X4),
@@ -132,6 +137,14 @@ def tile_picked_phmlp_relu_p_kernel(
                 start=True,
                 stop=True,
             )
-            result = keep.tile([N, QUARTER], F32, name=f"result{u}")
-            nc.scalar.copy(result[:], acc[:])
-            nc.sync.dma_start(out[:, u * QUARTER : (u + 1) * QUARTER], result[:])
+            result = keep.tile([N, width], F32, name=f"result{banks[0]}")
+            copy_out(result[:], acc[:])
+            quarters = out.rearrange("m (u n) -> m u n", n=QUARTER)
+            nc.sync.dma_start(
+                quarters[:, banks[0] : banks[-1] + 1 : 2, :], result[:].rearrange("m (s n) -> m s n", n=QUARTER)
+            )
+
+        h_even, h_one, h_three = relu_rounded([0, 2]), relu_rounded([1]), relu_rounded([3])
+        second_product([1], h_one, nc.scalar.copy)
+        second_product([0, 2], h_even, nc.scalar.copy)
+        second_product([3], h_three, nc.vector.tensor_copy)

@@ -24,7 +24,7 @@ GROUP = 16
 HALF = S // 2
 QUARTER = S // 4
 PLANE_STEP = 8
-M_VECTOR = 88
+M_VECTOR = (40, 88)
 
 
 def tile_picked_phmlp_relu_p_kernel(
@@ -49,34 +49,38 @@ def tile_picked_phmlp_relu_p_kernel(
         nc.vector.memset(scale_table[:].bitcast(I32), 0)
         scale_rows = x_scales.bitcast(I32).rearrange("z (g e) c -> e g z c", e=2)
         w1_raw = [keep.tile([P, PACK, H], F32, name=f"w1_raw{z}", align_bytes=256) for z in range(PASSES)]
-        nc.sync.dma_start(w1_raw[0][:, :2, :], w1_rows(0)[:, :2, :])
+        nc.sync.dma_start(w1_raw[0][:], w1_rows(0))
         nc.sync.dma_start(offsets[:], offs)
         for e in range(2):
             nc.sync.dma_start(scale_table[e:P:PLANE_STEP, :].bitcast(I32), scale_rows[e])
-        nc.sync.dma_start(w1_raw[0][:, 2:, :], w1_rows(0)[:, 2:, :])
         word_table = [load_words(0, "word_table0")]
         nc.sync.dma_start(w1_raw[1][:], w1_rows(1))
 
         picked_scales = keep.tile([P, S], U8, name="picked_scales", align_bytes=256)
         nc.vector.tensor_copy(picked_scales[:], scale_table[:].indirect(offsets[:]))
-        x_plane = keep.tile([P, S], U8, name="x_plane", align_bytes=64)
-        nc.vector.tensor_copy(x_plane[:].bitcast(I32), picked_scales[:].bitcast(I32))
+        x_plane = [keep.tile([P, S], U8, name=f"x_plane{z}", align_bytes=64) for z in range(PASSES)]
         for z in range(PASSES):
+            nc.vector.tensor_copy(x_plane[z][:].bitcast(I32), picked_scales[:].bitcast(I32))
+
+        def move_odd_rows(z):
             for e in range(2):
                 row = PLANE_STEP * z + e
                 nc.sync.dma_start(
-                    x_plane[row + 2 : P : QUADRANT, :].bitcast(I32),
-                    x_plane[row + GROUP : P : QUADRANT, :].bitcast(I32),
+                    x_plane[z][row + 2 : P : QUADRANT, :].bitcast(I32),
+                    x_plane[z][row + GROUP : P : QUADRANT, :].bitcast(I32),
                 )
+
+        move_odd_rows(0)
         word_table.append(load_words(1, "picked_scales"))
+        move_odd_rows(1)
 
         hidden = [psum.tile([P, PACK, QUARTER], F32, name=f"hidden{u}") for u in range(S // QUARTER)]
         for z in range(PASSES):
             grouped = keep.tile([P, PACK, P, PACK], BF16, name=f"w1_grouped{z}", align_bytes=64)
             rounded = grouped[:].rearrange("p t m j -> p m t j")
             exact = w1_raw[z][:].rearrange("p j (m t) -> p m t j", t=PACK)
-            nc.vector.tensor_copy(rounded[:, :M_VECTOR], exact[:, :M_VECTOR])
-            nc.scalar.activation(rounded[:, M_VECTOR:], exact[:, M_VECTOR:], COPY)
+            nc.vector.tensor_copy(rounded[:, : M_VECTOR[z]], exact[:, : M_VECTOR[z]])
+            nc.scalar.activation(rounded[:, M_VECTOR[z] :], exact[:, M_VECTOR[z] :], COPY)
             w1_codes = keep.tile([P, H], U32, name=f"w1_codes{z}", align_bytes=64)
             w1_plane = keep.tile([P, H], U8, name=f"w1_plane{z}", align_bytes=64)
             nc.vector.quantize_mx(
@@ -95,14 +99,14 @@ def tile_picked_phmlp_relu_p_kernel(
                             lhsT=w1_codes[:, t * P : (t + 1) * P].bitcast(FP8X4),
                             lhsT_scale=w1_plane[:, t * P : (t + 1) * P],
                             rhs=picked[:, v * QUARTER : (v + 1) * QUARTER].bitcast(FP8X4),
-                            rhs_scale=x_plane[PLANE_STEP * z :, u * QUARTER : (u + 1) * QUARTER],
+                            rhs_scale=x_plane[z][PLANE_STEP * z :, u * QUARTER : (u + 1) * QUARTER],
                             start=(z == 0 and t == 0),
                             stop=(z == PASSES - 1 and t == PACK - 1),
                         )
 
         w2_codes = keep.tile([P, N], I32, name="w2_codes", tag="w1_raw1", align_bytes=256)
         nc.sync.dma_start(w2_codes[:], w2_words[0].rearrange("p c j -> p (c j)").bitcast(I32))
-        w2_plane = keep.tile([P, N], U8, name="w2_plane", tag="w1_raw0", align_bytes=256)
+        w2_plane = keep.tile([P, N], U8, name="w2_plane", tag="word_table0", align_bytes=256)
         nc.gpsimd.memset(w2_plane[:].bitcast(I32), 0)
         for q in range(P // QUADRANT):
             nc.sync.dma_start(
@@ -110,24 +114,21 @@ def tile_picked_phmlp_relu_p_kernel(
                 w2_scales[0, 4 * q : 4 * q + 4, :].bitcast(I32),
             )
 
-        def relu_rounded(banks):
-            h = keep.tile([P, len(banks), QUARTER, PACK], BF16, name=f"h{banks[0]}", align_bytes=64)
-            for slot, u in enumerate(banks):
-                sums = hidden[u][:].rearrange("p t n -> p n t")
-                if u % 2 == 0:
-                    nc.vector.tensor_scalar_max(h[:, slot], sums, 0.0)
-                else:
-                    nc.scalar.activation(h[:, slot], sums, RELU)
-            return h
-
-        def second_product(banks, h, copy_out):
-            width = len(banks) * QUARTER
-            h_codes = keep.tile([P, width], U32, name=f"h_codes{banks[0]}", align_bytes=64)
-            h_plane = keep.tile([P, width], U8, name=f"h_plane{banks[0]}", align_bytes=64)
+        banks = range(S // QUARTER)
+        h = [keep.tile([P, QUARTER, PACK], BF16, name=f"h{u}", align_bytes=64) for u in banks]
+        for u in banks:
+            sums = hidden[u][:].rearrange("p t n -> p n t")
+            if u % 2 == 0:
+                nc.vector.tensor_scalar_max(h[u][:], sums, 0.0)
+            else:
+                nc.scalar.activation(h[u][:], sums, RELU)
+        for u in banks:
+            h_codes = keep.tile([P, QUARTER], U32, name=f"h_codes{u}", align_bytes=64)
+            h_plane = keep.tile([P, QUARTER], U8, name=f"h_plane{u}", align_bytes=64)
             nc.vector.quantize_mx(
-                out=h_codes[:].bitcast(FP8X4), scales=h_plane[:], in_=h[:].rearrange("p s n t -> p (s n t)")
+                out=h_codes[:].bitcast(FP8X4), scales=h_plane[:], in_=h[u][:].rearrange("p n t -> p (n t)")
             )
-            acc = psum.tile([N, width], F32, name=f"acc{banks[0]}")
+            acc = psum.tile([N, QUARTER], F32, name=f"acc{u}")
             nc.tensor.matmul_mx(
                 out=acc[:],
                 lhsT=w2_codes[:].bitcast(FP8X4),
@@ -137,14 +138,7 @@ def tile_picked_phmlp_relu_p_kernel(
                 start=True,
                 stop=True,
             )
-            result = keep.tile([N, width], F32, name=f"result{banks[0]}")
+            result = keep.tile([N, QUARTER], F32, name=f"result{u}")
+            copy_out = nc.vector.tensor_copy if u == banks[-1] else nc.scalar.copy
             copy_out(result[:], acc[:])
-            quarters = out.rearrange("m (u n) -> m u n", n=QUARTER)
-            nc.sync.dma_start(
-                quarters[:, banks[0] : banks[-1] + 1 : 2, :], result[:].rearrange("m (s n) -> m s n", n=QUARTER)
-            )
-
-        h_even, h_one, h_three = relu_rounded([0, 2]), relu_rounded([1]), relu_rounded([3])
-        second_product([1], h_one, nc.scalar.copy)
-        second_product([0, 2], h_even, nc.scalar.copy)
-        second_product([3], h_three, nc.vector.tensor_copy)
+            nc.sync.dma_start(out[:, u * QUARTER : (u + 1) * QUARTER], result[:])

@@ -24,7 +24,7 @@ GROUP = 16
 HALF = S // 2
 QUARTER = S // 4
 PLANE_STEP = 8
-M_VECTOR = (40, 88)
+M_VECTOR = 80
 
 
 def tile_picked_phmlp_relu_p_kernel(
@@ -38,10 +38,8 @@ def tile_picked_phmlp_relu_p_kernel(
         def w1_rows(z):
             return w1[z * K_PASS : (z + 1) * K_PASS, :].rearrange("(p j) c -> p j c", j=PACK)
 
-        def load_words(z, tag):
-            table = keep.tile([P, T], I32, name=f"word_table{z}", tag=tag, align_bytes=256)
-            nc.sync.dma_start(table[:], x_words[z].rearrange("p c j -> p (c j)").bitcast(I32))
-            return table
+        def word_rows(z):
+            return x_words[z].rearrange("p c j -> p (c j)").bitcast(I32)
 
         offsets = keep.tile([P, S // GROUP], U16, name="offsets")
 
@@ -49,12 +47,14 @@ def tile_picked_phmlp_relu_p_kernel(
         nc.vector.memset(scale_table[:].bitcast(I32), 0)
         scale_rows = x_scales.bitcast(I32).rearrange("z (g e) c -> e g z c", e=2)
         w1_raw = [keep.tile([P, PACK, H], F32, name=f"w1_raw{z}", align_bytes=256) for z in range(PASSES)]
-        nc.sync.dma_start(w1_raw[0][:], w1_rows(0))
+        word_table = [keep.tile([P, T], I32, name="word_table0", align_bytes=256)]
+        nc.sync.dma_start(word_table[0][:, : T // 2], word_rows(0)[:, : T // 2])
         nc.sync.dma_start(offsets[:], offs)
         for e in range(2):
             nc.sync.dma_start(scale_table[e:P:PLANE_STEP, :].bitcast(I32), scale_rows[e])
-        word_table = [load_words(0, "word_table0")]
-        nc.sync.dma_start(w1_raw[1][:], w1_rows(1))
+        nc.sync.dma_start(word_table[0][:, T // 2 :], word_rows(0)[:, T // 2 :])
+        for z in range(PASSES):
+            nc.sync.dma_start(w1_raw[z][:], w1_rows(z))
 
         picked_scales = keep.tile([P, S], U8, name="picked_scales", align_bytes=256)
         nc.vector.tensor_copy(picked_scales[:], scale_table[:].indirect(offsets[:]))
@@ -71,16 +71,17 @@ def tile_picked_phmlp_relu_p_kernel(
                 )
 
         move_odd_rows(0)
-        word_table.append(load_words(1, "picked_scales"))
+        word_table.append(keep.tile([P, T], I32, name="word_table1", tag="picked_scales", align_bytes=256))
+        nc.sync.dma_start(word_table[1][:], word_rows(1))
         move_odd_rows(1)
 
         hidden = [psum.tile([P, PACK, QUARTER], F32, name=f"hidden{u}") for u in range(S // QUARTER)]
         for z in range(PASSES):
-            grouped = keep.tile([P, PACK, P, PACK], BF16, name=f"w1_grouped{z}", align_bytes=64)
+            grouped = keep.tile([P, PACK, P, PACK], BF16, name=f"w1_grouped{z}", tag="w1_grouped", align_bytes=64)
             rounded = grouped[:].rearrange("p t m j -> p m t j")
             exact = w1_raw[z][:].rearrange("p j (m t) -> p m t j", t=PACK)
-            nc.vector.tensor_copy(rounded[:, : M_VECTOR[z]], exact[:, : M_VECTOR[z]])
-            nc.scalar.activation(rounded[:, M_VECTOR[z] :], exact[:, M_VECTOR[z] :], COPY)
+            nc.vector.tensor_copy(rounded[:, :M_VECTOR], exact[:, :M_VECTOR])
+            nc.scalar.activation(rounded[:, M_VECTOR:], exact[:, M_VECTOR:], COPY)
             w1_codes = keep.tile([P, H], U32, name=f"w1_codes{z}", align_bytes=64)
             w1_plane = keep.tile([P, H], U8, name=f"w1_plane{z}", align_bytes=64)
             nc.vector.quantize_mx(
@@ -104,10 +105,10 @@ def tile_picked_phmlp_relu_p_kernel(
                             stop=(z == PASSES - 1 and t == PACK - 1),
                         )
 
-        w2_codes = keep.tile([P, N], I32, name="w2_codes", tag="w1_raw1", align_bytes=256)
+        w2_codes = keep.tile([P, N], I32, name="w2_codes", tag="word_table0", align_bytes=256)
         nc.sync.dma_start(w2_codes[:], w2_words[0].rearrange("p c j -> p (c j)").bitcast(I32))
-        w2_plane = keep.tile([P, N], U8, name="w2_plane", tag="word_table0", align_bytes=256)
-        nc.gpsimd.memset(w2_plane[:].bitcast(I32), 0)
+        w2_plane = keep.tile([P, N], U8, name="w2_plane", tag="w1_raw0", align_bytes=256)
+        nc.vector.memset(w2_plane[:].bitcast(I32), 0)
         for q in range(P // QUADRANT):
             nc.sync.dma_start(
                 w2_plane[QUADRANT * q : QUADRANT * q + 4, :].bitcast(I32),

@@ -88,6 +88,19 @@ def tile_picked_phmlp_relu_p_kernel(
                 out=w1_codes[:].bitcast(FP8X4), scales=w1_plane[:], in_=grouped[:].rearrange("p t m j -> p (t m j)")
             )
 
+            if z == PASSES - 1:
+                unread = psum.tile([P, H], F32, name="unread", tag="acc0")
+                for t in range(2):
+                    nc.tensor.matmul_mx(
+                        out=unread[:],
+                        lhsT=w1_codes[:, t * P : (t + 1) * P].bitcast(FP8X4),
+                        lhsT_scale=w1_plane[:, t * P : (t + 1) * P],
+                        rhs=w1_codes[:].bitcast(FP8X4),
+                        rhs_scale=w1_plane[:],
+                        start=True,
+                        stop=True,
+                    )
+
             for half in range(S // HALF):
                 picked = keep.tile([P, HALF], U32, name=f"picked{z}_{half}", align_bytes=64)
                 entries = offsets[:, half * HALF // GROUP : (half + 1) * HALF // GROUP]

@@ -88,7 +88,7 @@ def tile_picked_phmlp_relu_p_kernel(
                 out=w1_codes[:].bitcast(FP8X4), scales=w1_plane[:], in_=grouped[:].rearrange("p t m j -> p (t m j)")
             )
 
-            if z == PASSES - 1:
+            if z == 0:
                 unread = psum.tile([P, H], F32, name="unread", tag="acc0")
                 for t in range(2):
                     nc.tensor.matmul_mx(

@@ -24,6 +24,7 @@ GROUP = 16
 HALF = S // 2
 QUARTER = S // 4
 PLANE_STEP = 8
+WARM_UP_WIDTHS = (H, H, P)
 M_VECTOR = 80
 
 
@@ -52,9 +53,9 @@ def tile_picked_phmlp_relu_p_kernel(
         nc.sync.dma_start(offsets[:], offs)
         for e in range(2):
             nc.sync.dma_start(scale_table[e:P:PLANE_STEP, :].bitcast(I32), scale_rows[e])
+        nc.sync.dma_start(w1_raw[0][:], w1_rows(0))
         nc.sync.dma_start(word_table[0][:, T // 2 :], word_rows(0)[:, T // 2 :])
-        for z in range(PASSES):
-            nc.sync.dma_start(w1_raw[z][:], w1_rows(z))
+        nc.sync.dma_start(w1_raw[1][:], w1_rows(1))
 
         picked_scales = keep.tile([P, S], U8, name="picked_scales", align_bytes=256)
         nc.vector.tensor_copy(picked_scales[:], scale_table[:].indirect(offsets[:]))
@@ -77,7 +78,7 @@ def tile_picked_phmlp_relu_p_kernel(
 
         hidden = [psum.tile([P, PACK, QUARTER], F32, name=f"hidden{u}") for u in range(S // QUARTER)]
         for z in range(PASSES):
-            grouped = keep.tile([P, PACK, P, PACK], BF16, name=f"w1_grouped{z}", tag="w1_grouped", align_bytes=64)
+            grouped = keep.tile([P, PACK, P, PACK], BF16, name=f"w1_grouped{z}", align_bytes=64)
             rounded = grouped[:].rearrange("p t m j -> p m t j")
             exact = w1_raw[z][:].rearrange("p j (m t) -> p m t j", t=PACK)
             nc.vector.tensor_copy(rounded[:, :M_VECTOR], exact[:, :M_VECTOR])
@@ -90,21 +91,22 @@ def tile_picked_phmlp_relu_p_kernel(
 
             if z == 0:
                 unread = psum.tile([P, H], F32, name="unread", tag="acc0")
-                for t in range(2):
+                for t, width in enumerate(WARM_UP_WIDTHS):
                     nc.tensor.matmul_mx(
-                        out=unread[:],
+                        out=unread[:, :width],
                         lhsT=w1_codes[:, t * P : (t + 1) * P].bitcast(FP8X4),
                         lhsT_scale=w1_plane[:, t * P : (t + 1) * P],
-                        rhs=w1_codes[:].bitcast(FP8X4),
-                        rhs_scale=w1_plane[:],
+                        rhs=w1_codes[:, :width].bitcast(FP8X4),
+                        rhs_scale=w1_plane[:, :width],
                         start=True,
                         stop=True,
                     )
 
+            gathered = keep.tile([P, S], U32, name=f"picked{z}", tag=("w1_grouped0", "picked1")[z], align_bytes=64)
             for half in range(S // HALF):
-                picked = keep.tile([P, HALF], U32, name=f"picked{z}_{half}", align_bytes=64)
+                picked = gathered[:, half * HALF : (half + 1) * HALF]
                 entries = offsets[:, half * HALF // GROUP : (half + 1) * HALF // GROUP]
-                nc.vector.tensor_copy(picked[:], word_table[z][:].bitcast(U32).indirect(entries))
+                nc.vector.tensor_copy(picked, word_table[z][:].bitcast(U32).indirect(entries))
                 for v in range(HALF // QUARTER):
                     u = half * HALF // QUARTER + v
                     for t in range(PACK):

@@ -24,7 +24,8 @@ GROUP = 16
 HALF = S // 2
 QUARTER = S // 4
 PLANE_STEP = 8
-WARM_UP_WIDTHS = (H, H, P)
+WARM_UPS = 3
+WARM_UP_ROWS = 64
 M_VECTOR = 80
 
 
@@ -91,13 +92,13 @@ def tile_picked_phmlp_relu_p_kernel(
 
             if z == 0:
                 unread = psum.tile([P, H], F32, name="unread", tag="acc0")
-                for t, width in enumerate(WARM_UP_WIDTHS):
+                for t in range(WARM_UPS):
                     nc.tensor.matmul_mx(
-                        out=unread[:, :width],
-                        lhsT=w1_codes[:, t * P : (t + 1) * P].bitcast(FP8X4),
-                        lhsT_scale=w1_plane[:, t * P : (t + 1) * P],
-                        rhs=w1_codes[:, :width].bitcast(FP8X4),
-                        rhs_scale=w1_plane[:, :width],
+                        out=unread[:WARM_UP_ROWS, :],
+                        lhsT=w1_codes[:, t * P : t * P + WARM_UP_ROWS].bitcast(FP8X4),
+                        lhsT_scale=w1_plane[:, t * P : t * P + WARM_UP_ROWS],
+                        rhs=w1_codes[:].bitcast(FP8X4),
+                        rhs_scale=w1_plane[:],
                         start=True,
                         stop=True,
                     )

@@ -24,8 +24,6 @@ GROUP = 16
 HALF = S // 2
 QUARTER = S // 4
 PLANE_STEP = 8
-WARM_UPS = 3
-WARM_UP_ROWS = 64
 M_VECTOR = 80
 
 
@@ -89,19 +87,6 @@ def tile_picked_phmlp_relu_p_kernel(
             nc.vector.quantize_mx(
                 out=w1_codes[:].bitcast(FP8X4), scales=w1_plane[:], in_=grouped[:].rearrange("p t m j -> p (t m j)")
             )
-
-            if z == 0:
-                unread = psum.tile([P, H], F32, name="unread", tag="acc0")
-                for t in range(WARM_UPS):
-                    nc.tensor.matmul_mx(
-                        out=unread[:WARM_UP_ROWS, :],
-                        lhsT=w1_codes[:, t * P : t * P + WARM_UP_ROWS].bitcast(FP8X4),
-                        lhsT_scale=w1_plane[:, t * P : t * P + WARM_UP_ROWS],
-                        rhs=w1_codes[:].bitcast(FP8X4),
-                        rhs_scale=w1_plane[:],
-                        start=True,
-                        stop=True,
-                    )
 
             gathered = keep.tile([P, S], U32, name=f"picked{z}", tag=("w1_grouped0", "picked1")[z], align_bytes=64)
             for half in range(S // HALF):

@@ -17,6 +17,7 @@ RELU = mybir.ActivationFunctionType.Relu
 
 P = 128
 PACK = 4
+PAIR = PACK // 2
 K_PASS = P * PACK
 PASSES = K // K_PASS
 QUADRANT = 32
@@ -33,6 +34,7 @@ def tile_picked_phmlp_relu_p_kernel(
     nc = tc.nc
     with ExitStack() as ctx:
         keep = ctx.enter_context(tc.tile_pool(name="keep", bufs=1))
+        held = ctx.enter_context(tc.tile_pool(name="held", bufs=1))
         psum = ctx.enter_context(tc.psum_pool(name="psum", bufs=1))
 
         def w1_rows(z):
@@ -46,17 +48,18 @@ def tile_picked_phmlp_relu_p_kernel(
         scale_table = keep.tile([P, T], U8, name="scale_table", align_bytes=256)
         nc.vector.memset(scale_table[:].bitcast(I32), 0)
         scale_rows = x_scales.bitcast(I32).rearrange("z (g e) c -> e g z c", e=2)
-        w1_raw = [keep.tile([P, PACK, H], F32, name=f"w1_raw{z}", align_bytes=256) for z in range(PASSES)]
+        w1_raw0 = keep.tile([P, PACK, H], F32, name="w1_raw0", align_bytes=256)
+        w1_raw1 = [keep.tile([P, PAIR, H], F32, name="w1_raw1a", align_bytes=256)]
         word_table = [keep.tile([P, T], I32, name="word_table0", align_bytes=256)]
         nc.sync.dma_start(word_table[0][:, : T // 2], word_rows(0)[:, : T // 2])
         nc.sync.dma_start(offsets[:], offs)
         for e in range(2):
             nc.sync.dma_start(scale_table[e:P:PLANE_STEP, :].bitcast(I32), scale_rows[e])
-        nc.sync.dma_start(w1_raw[0][:], w1_rows(0))
+        nc.sync.dma_start(w1_raw0[:], w1_rows(0))
         nc.sync.dma_start(word_table[0][:, T // 2 :], word_rows(0)[:, T // 2 :])
-        nc.sync.dma_start(w1_raw[1][:], w1_rows(1))
+        nc.sync.dma_start(w1_raw1[0][:], w1_rows(1)[:, :PAIR])
 
-        picked_scales = keep.tile([P, S], U8, name="picked_scales", align_bytes=256)
+        picked_scales = held.tile([P, S], U8, name="picked_scales", align_bytes=256, offset=PAIR * H * 4 - S // 2)
         nc.vector.tensor_copy(picked_scales[:], scale_table[:].indirect(offsets[:]))
         x_plane = [keep.tile([P, S], U8, name=f"x_plane{z}", align_bytes=64) for z in range(PASSES)]
         for z in range(PASSES):
@@ -71,7 +74,9 @@ def tile_picked_phmlp_relu_p_kernel(
                 )
 
         move_odd_rows(0)
-        word_table.append(keep.tile([P, T], I32, name="word_table1", tag="picked_scales", align_bytes=256))
+        w1_raw1.append(held.tile([P, PAIR, H], F32, name="w1_raw1b", align_bytes=256, offset=0))
+        nc.sync.dma_start(w1_raw1[1][:], w1_rows(1)[:, PAIR:])
+        word_table.append(held.tile([P, T], I32, name="word_table1", align_bytes=256, offset=PAIR * H * 4))
         nc.sync.dma_start(word_table[1][:], word_rows(1))
         move_odd_rows(1)
 
@@ -79,20 +84,25 @@ def tile_picked_phmlp_relu_p_kernel(
         for z in range(PASSES):
             grouped = keep.tile([P, PACK, P, PACK], BF16, name=f"w1_grouped{z}", align_bytes=64)
             rounded = grouped[:].rearrange("p t m j -> p m t j")
-            exact = w1_raw[z][:].rearrange("p j (m t) -> p m t j", t=PACK)
-            nc.vector.tensor_copy(rounded[:, :M_VECTOR], exact[:, :M_VECTOR])
-            nc.scalar.activation(rounded[:, M_VECTOR:], exact[:, M_VECTOR:], COPY)
+            if z == 0:
+                exact = w1_raw0[:].rearrange("p j (m t) -> p m t j", t=PACK)
+                nc.vector.tensor_copy(rounded[:, :M_VECTOR], exact[:, :M_VECTOR])
+                nc.scalar.activation(rounded[:, M_VECTOR:], exact[:, M_VECTOR:], COPY)
+            else:
+                early, late = [raw[:].rearrange("p j (m t) -> p m t j", t=PACK) for raw in w1_raw1]
+                nc.scalar.activation(rounded[:, :, :, :PAIR], early, COPY)
+                nc.vector.tensor_copy(rounded[:, :, :, PAIR:], late)
             w1_codes = keep.tile([P, H], U32, name=f"w1_codes{z}", align_bytes=64)
             w1_plane = keep.tile([P, H], U8, name=f"w1_plane{z}", align_bytes=64)
             nc.vector.quantize_mx(
                 out=w1_codes[:].bitcast(FP8X4), scales=w1_plane[:], in_=grouped[:].rearrange("p t m j -> p (t m j)")
             )
 
-            gathered = keep.tile([P, S], U32, name=f"picked{z}", tag=("w1_grouped0", "picked1")[z], align_bytes=64)
             for half in range(S // HALF):
-                picked = gathered[:, half * HALF : (half + 1) * HALF]
+                tag = "w1_grouped0" if (z, half) == (0, 1) else f"picked{z}_{half}"
+                picked = keep.tile([P, HALF], U32, name=f"picked{z}_{half}", tag=tag, align_bytes=64)
                 entries = offsets[:, half * HALF // GROUP : (half + 1) * HALF // GROUP]
-                nc.vector.tensor_copy(picked, word_table[z][:].bitcast(U32).indirect(entries))
+                nc.vector.tensor_copy(picked[:], word_table[z][:].bitcast(U32).indirect(entries))
                 for v in range(HALF // QUARTER):
                     u = half * HALF // QUARTER + v
                     for t in range(PACK):

@@ -98,6 +98,19 @@ def tile_picked_phmlp_relu_p_kernel(
                 out=w1_codes[:].bitcast(FP8X4), scales=w1_plane[:], in_=grouped[:].rearrange("p t m j -> p (t m j)")
             )
 
+            if z == PASSES - 1:
+                unread = psum.tile([P, H], F32, name="unread", tag="acc0")
+                for t in range(2):
+                    nc.tensor.matmul_mx(
+                        out=unread[:],
+                        lhsT=w1_codes[:, t * P : (t + 1) * P].bitcast(FP8X4),
+                        lhsT_scale=w1_plane[:, t * P : (t + 1) * P],
+                        rhs=w1_codes[:].bitcast(FP8X4),
+                        rhs_scale=w1_plane[:],
+                        start=True,
+                        stop=True,
+                    )
+
             for half in range(S // HALF):
                 tag = "w1_grouped0" if (z, half) == (0, 1) else f"picked{z}_{half}"
                 picked = keep.tile([P, HALF], U32, name=f"picked{z}_{half}", tag=tag, align_bytes=64)

@@ -81,6 +81,7 @@ def tile_picked_phmlp_relu_p_kernel(
         move_odd_rows(1)
 
         hidden = [psum.tile([P, PACK, QUARTER], F32, name=f"hidden{u}") for u in range(S // QUARTER)]
+        quantised = []
         for z in range(PASSES):
             grouped = keep.tile([P, PACK, P, PACK], BF16, name=f"w1_grouped{z}", align_bytes=64)
             rounded = grouped[:].rearrange("p t m j -> p m t j")
@@ -94,19 +95,26 @@ def tile_picked_phmlp_relu_p_kernel(
                 nc.vector.tensor_copy(rounded[:, :, :, PAIR:], late)
             w1_codes = keep.tile([P, H], U32, name=f"w1_codes{z}", align_bytes=64)
             w1_plane = keep.tile([P, H], U8, name=f"w1_plane{z}", align_bytes=64)
-            nc.vector.quantize_mx(
-                out=w1_codes[:].bitcast(FP8X4), scales=w1_plane[:], in_=grouped[:].rearrange("p t m j -> p (t m j)")
-            )
+            pieces = 1 + z
+            for i in range(pieces):
+                cols = slice(i * H // pieces, (i + 1) * H // pieces)
+                tiles = slice(i * PACK // pieces, (i + 1) * PACK // pieces)
+                nc.vector.quantize_mx(
+                    out=w1_codes[:, cols].bitcast(FP8X4),
+                    scales=w1_plane[:, cols],
+                    in_=grouped[:, tiles].rearrange("p t m j -> p (t m j)"),
+                )
+            quantised.append((w1_codes, w1_plane))
 
             if z == PASSES - 1:
                 unread = psum.tile([P, H], F32, name="unread", tag="acc0")
-                for t in range(2):
+                for width in (P, P, QUADRANT):
                     nc.tensor.matmul_mx(
-                        out=unread[:],
-                        lhsT=w1_codes[:, t * P : (t + 1) * P].bitcast(FP8X4),
-                        lhsT_scale=w1_plane[:, t * P : (t + 1) * P],
-                        rhs=w1_codes[:].bitcast(FP8X4),
-                        rhs_scale=w1_plane[:],
+                        out=unread[:width],
+                        lhsT=w1_codes[:, :width].bitcast(FP8X4),
+                        lhsT_scale=w1_plane[:, :width],
+                        rhs=quantised[0][0][:].bitcast(FP8X4),
+                        rhs_scale=quantised[0][1][:],
                         start=True,
                         stop=True,
                     )

@@ -85,30 +85,36 @@ def tile_picked_phmlp_relu_p_kernel(
         for z in range(PASSES):
             grouped = keep.tile([P, PACK, P, PACK], BF16, name=f"w1_grouped{z}", align_bytes=64)
             rounded = grouped[:].rearrange("p t m j -> p m t j")
+            w1_codes = keep.tile([P, H], U32, name=f"w1_codes{z}", align_bytes=64)
+            w1_plane = keep.tile([P, H], U8, name=f"w1_plane{z}", align_bytes=64)
+
+            def quantise(cols):
+                nc.vector.quantize_mx(
+                    out=w1_codes[:, cols].bitcast(FP8X4),
+                    scales=w1_plane[:, cols],
+                    in_=grouped[:].rearrange("p t m j -> p (t m j)")[:, PACK * cols.start : PACK * cols.stop],
+                )
+
             if z == 0:
                 exact = w1_raw0[:].rearrange("p j (m t) -> p m t j", t=PACK)
                 nc.vector.tensor_copy(rounded[:, :M_VECTOR], exact[:, :M_VECTOR])
                 nc.scalar.activation(rounded[:, M_VECTOR:], exact[:, M_VECTOR:], COPY)
+                quantise(slice(0, H))
             else:
                 early, late = [raw[:].rearrange("p j (m t) -> p m t j", t=PACK) for raw in w1_raw1]
-                nc.scalar.activation(rounded[:, :, :, :PAIR], early, COPY)
-                nc.vector.tensor_copy(rounded[:, :, :, PAIR:], late)
-            w1_codes = keep.tile([P, H], U32, name=f"w1_codes{z}", align_bytes=64)
-            w1_plane = keep.tile([P, H], U8, name=f"w1_plane{z}", align_bytes=64)
-            pieces = 1 + z
-            for i in range(pieces):
-                cols = slice(i * H // pieces, (i + 1) * H // pieces)
-                tiles = slice(i * PACK // pieces, (i + 1) * PACK // pieces)
-                nc.vector.quantize_mx(
-                    out=w1_codes[:, cols].bitcast(FP8X4),
-                    scales=w1_plane[:, cols],
-                    in_=grouped[:, tiles].rearrange("p t m j -> p (t m j)"),
-                )
+                for m in (slice(0, 64), slice(64, P)):
+                    nc.scalar.activation(rounded[:, m, :, :PAIR], early[:, m], COPY)
+                for m in (slice(0, 64), slice(64, 96)):
+                    nc.vector.tensor_copy(rounded[:, m, :, PAIR:], late[:, m])
+                quantise(slice(0, 64))
+                nc.vector.tensor_copy(rounded[:, 96:, :, PAIR:], late[:, 96:])
+                for cols in (slice(64, P), slice(P, 2 * P), slice(2 * P, H)):
+                    quantise(cols)
             quantised.append((w1_codes, w1_plane))
 
             if z == PASSES - 1:
                 unread = psum.tile([P, H], F32, name="unread", tag="acc0")
-                for width in (P, P, QUADRANT):
+                for width in (64, 64, 64):
                     nc.tensor.matmul_mx(
                         out=unread[:width],
                         lhsT=w1_codes[:, :width].bitcast(FP8X4),

@@ -26,6 +26,8 @@ HALF = S // 2
 QUARTER = S // 4
 PLANE_STEP = 8
 M_VECTOR = 80
+WARM_UPS = 3
+WARM_WIDTH = 32
 
 
 def tile_picked_phmlp_relu_p_kernel(
@@ -114,11 +116,11 @@ def tile_picked_phmlp_relu_p_kernel(
 
             if z == PASSES - 1:
                 unread = psum.tile([P, H], F32, name="unread", tag="acc0")
-                for width in (64, 64, 64):
+                for warm_up in range(WARM_UPS):
                     nc.tensor.matmul_mx(
-                        out=unread[:width],
-                        lhsT=w1_codes[:, :width].bitcast(FP8X4),
-                        lhsT_scale=w1_plane[:, :width],
+                        out=unread[:WARM_WIDTH],
+                        lhsT=w1_codes[:, :WARM_WIDTH].bitcast(FP8X4),
+                        lhsT_scale=w1_plane[:, :WARM_WIDTH],
                         rhs=quantised[0][0][:].bitcast(FP8X4),
                         rhs_scale=quantised[0][1][:],
                         start=True,
@@ -155,19 +157,24 @@ def tile_picked_phmlp_relu_p_kernel(
 
         banks = range(S // QUARTER)
         h = [keep.tile([P, QUARTER, PACK], BF16, name=f"h{u}", align_bytes=64) for u in banks]
-        for u in banks:
-            sums = hidden[u][:].rearrange("p t n -> p n t")
-            if u % 2 == 0:
-                nc.vector.tensor_scalar_max(h[u][:], sums, 0.0)
+        result = [keep.tile([N, QUARTER], F32, name=f"result{u}") for u in banks]
+        sums = {}
+
+        def activate(engine, u, cols):
+            source = hidden[u][:, :, cols].rearrange("p t n -> p n t")
+            if engine is nc.vector:
+                nc.vector.tensor_scalar_max(h[u][:, cols, :], source, 0.0)
             else:
-                nc.scalar.activation(h[u][:], sums, RELU)
-        for u in banks:
-            h_codes = keep.tile([P, QUARTER], U32, name=f"h_codes{u}", align_bytes=64)
-            h_plane = keep.tile([P, QUARTER], U8, name=f"h_plane{u}", align_bytes=64)
+                nc.scalar.activation(h[u][:, cols, :], source, RELU)
+
+        def multiply(u, cols, tag):
+            width = cols.stop - cols.start
+            h_codes = keep.tile([P, width], U32, name=f"h_codes{u}_{cols.start}", align_bytes=64)
+            h_plane = keep.tile([P, width], U8, name=f"h_plane{u}_{cols.start}", align_bytes=64)
             nc.vector.quantize_mx(
-                out=h_codes[:].bitcast(FP8X4), scales=h_plane[:], in_=h[u][:].rearrange("p n t -> p (n t)")
+                out=h_codes[:].bitcast(FP8X4), scales=h_plane[:], in_=h[u][:, cols, :].rearrange("p n t -> p (n t)")
             )
-            acc = psum.tile([N, QUARTER], F32, name=f"acc{u}")
+            acc = psum.tile([N, width], F32, name=f"acc{u}_{cols.start}", tag=tag)
             nc.tensor.matmul_mx(
                 out=acc[:],
                 lhsT=w2_codes[:].bitcast(FP8X4),
@@ -177,7 +184,27 @@ def tile_picked_phmlp_relu_p_kernel(
                 start=True,
                 stop=True,
             )
-            result = keep.tile([N, QUARTER], F32, name=f"result{u}")
-            copy_out = nc.vector.tensor_copy if u == banks[-1] else nc.scalar.copy
-            copy_out(result[:], acc[:])
-            nc.sync.dma_start(out[:, u * QUARTER : (u + 1) * QUARTER], result[:])
+            sums[u, cols.start] = acc
+
+        def copy_out(engine, u, cols):
+            copy = nc.vector.tensor_copy if engine is nc.vector else nc.scalar.copy
+            copy(result[u][:, cols], sums[u, cols.start][:])
+            if cols.stop == QUARTER:
+                nc.sync.dma_start(out[:, u * QUARTER : (u + 1) * QUARTER], result[u][:])
+
+        whole, low, high = slice(0, QUARTER), slice(0, QUARTER // 2), slice(QUARTER // 2, QUARTER)
+        activate(nc.scalar, 0, whole)
+        activate(nc.vector, 1, whole)
+        activate(nc.scalar, 2, whole)
+        activate(nc.scalar, 3, low)
+        activate(nc.scalar, 3, high)
+        multiply(0, whole, "acc0")
+        multiply(1, whole, "acc1")
+        multiply(2, whole, "acc2")
+        multiply(3, low, "acc3")
+        multiply(3, high, "hidden0")
+        copy_out(nc.scalar, 0, whole)
+        copy_out(nc.scalar, 1, whole)
+        copy_out(nc.scalar, 2, whole)
+        copy_out(nc.vector, 3, low)
+        copy_out(nc.vector, 3, high)

@@ -26,6 +26,10 @@ HALF = S // 2
 QUARTER = S // 4
 PLANE_STEP = 8
 M_VECTOR = 80
+FIRST = 768
+M_EARLY = 96
+M_LATE = 88
+LEAD = 64
 WARM_UPS = 3
 WARM_WIDTH = 32
 
@@ -53,12 +57,12 @@ def tile_picked_phmlp_relu_p_kernel(
         w1_raw0 = keep.tile([P, PACK, H], F32, name="w1_raw0", align_bytes=256)
         w1_raw1 = [keep.tile([P, PAIR, H], F32, name="w1_raw1a", align_bytes=256)]
         word_table = [keep.tile([P, T], I32, name="word_table0", align_bytes=256)]
-        nc.sync.dma_start(word_table[0][:, : T // 2], word_rows(0)[:, : T // 2])
+        nc.sync.dma_start(word_table[0][:, :FIRST], word_rows(0)[:, :FIRST])
         nc.sync.dma_start(offsets[:], offs)
         for e in range(2):
             nc.sync.dma_start(scale_table[e:P:PLANE_STEP, :].bitcast(I32), scale_rows[e])
         nc.sync.dma_start(w1_raw0[:], w1_rows(0))
-        nc.sync.dma_start(word_table[0][:, T // 2 :], word_rows(0)[:, T // 2 :])
+        nc.sync.dma_start(word_table[0][:, FIRST:], word_rows(0)[:, FIRST:])
         nc.sync.dma_start(w1_raw1[0][:], w1_rows(1)[:, :PAIR])
 
         picked_scales = held.tile([P, S], U8, name="picked_scales", align_bytes=256, offset=PAIR * H * 4 - S // 2)
@@ -104,13 +108,12 @@ def tile_picked_phmlp_relu_p_kernel(
                 quantise(slice(0, H))
             else:
                 early, late = [raw[:].rearrange("p j (m t) -> p m t j", t=PACK) for raw in w1_raw1]
-                for m in (slice(0, 64), slice(64, P)):
-                    nc.scalar.activation(rounded[:, m, :, :PAIR], early[:, m], COPY)
-                for m in (slice(0, 64), slice(64, 96)):
+                nc.scalar.activation(rounded[:, :M_EARLY, :, :PAIR], early[:, :M_EARLY], COPY)
+                nc.vector.tensor_copy(rounded[:, M_EARLY:, :, :PAIR], early[:, M_EARLY:])
+                nc.scalar.activation(rounded[:, M_LATE:, :, PAIR:], late[:, M_LATE:], COPY)
+                for m in (slice(0, LEAD), slice(LEAD, M_LATE)):
                     nc.vector.tensor_copy(rounded[:, m, :, PAIR:], late[:, m])
-                quantise(slice(0, 64))
-                nc.vector.tensor_copy(rounded[:, 96:, :, PAIR:], late[:, 96:])
-                for cols in (slice(64, P), slice(P, 2 * P), slice(2 * P, H)):
+                for cols in (slice(0, LEAD), slice(LEAD, P), slice(P, 2 * P), slice(2 * P, H)):
                     quantise(cols)
             quantised.append((w1_codes, w1_plane))
 

@@ -26,7 +26,7 @@ HALF = S // 2
 QUARTER = S // 4
 PLANE_STEP = 8
 M_VECTOR = 80
-FIRST = 768
+FIRST = 640
 M_EARLY = 96
 M_LATE = 88
 LEAD = 64
@@ -67,9 +67,12 @@ def tile_picked_phmlp_relu_p_kernel(
 
         picked_scales = held.tile([P, S], U8, name="picked_scales", align_bytes=256, offset=PAIR * H * 4 - S // 2)
         nc.vector.tensor_copy(picked_scales[:], scale_table[:].indirect(offsets[:]))
-        x_plane = [keep.tile([P, S], U8, name=f"x_plane{z}", align_bytes=64) for z in range(PASSES)]
-        for z in range(PASSES):
-            nc.vector.tensor_copy(x_plane[z][:].bitcast(I32), picked_scales[:].bitcast(I32))
+        x_planes = keep.tile([P, PASSES, S], U8, name="x_planes", align_bytes=64)
+        nc.vector.tensor_copy(
+            x_planes[:].bitcast(I32),
+            picked_scales[:].bitcast(I32).unsqueeze(1).to_broadcast([P, PASSES, S // PACK]),
+        )
+        x_plane = [x_planes[:, z, :] for z in range(PASSES)]
 
         def move_odd_rows(z):
             for e in range(2):

@@ -26,7 +26,7 @@ HALF = S // 2
 QUARTER = S // 4
 PLANE_STEP = 8
 M_VECTOR = 80
-FIRST = 640
+FIRST = 512
 M_EARLY = 96
 M_LATE = 88
 LEAD = 64

@@ -26,7 +26,7 @@ HALF = S // 2
 QUARTER = S // 4
 PLANE_STEP = 8
 M_VECTOR = 80
-FIRST = 512
+FIRST = 576
 M_EARLY = 96
 M_LATE = 88
 LEAD = 64

@@ -28,7 +28,7 @@ PLANE_STEP = 8
 M_VECTOR = 80
 FIRST = 576
 M_EARLY = 96
-M_LATE = 88
+M_LATE = 40
 LEAD = 64
 WARM_UPS = 3
 WARM_WIDTH = 32
@@ -66,12 +66,16 @@ def tile_picked_phmlp_relu_p_kernel(
         nc.sync.dma_start(w1_raw1[0][:], w1_rows(1)[:, :PAIR])
 
         picked_scales = held.tile([P, S], U8, name="picked_scales", align_bytes=256, offset=PAIR * H * 4 - S // 2)
-        nc.vector.tensor_copy(picked_scales[:], scale_table[:].indirect(offsets[:]))
+        halves = [slice(half * HALF, (half + 1) * HALF) for half in range(S // HALF)]
+        for places in halves:
+            entries = offsets[:, places.start // GROUP : places.stop // GROUP]
+            nc.vector.tensor_copy(picked_scales[:, places], scale_table[:].indirect(entries))
         x_planes = keep.tile([P, PASSES, S], U8, name="x_planes", align_bytes=64)
-        nc.vector.tensor_copy(
-            x_planes[:].bitcast(I32),
-            picked_scales[:].bitcast(I32).unsqueeze(1).to_broadcast([P, PASSES, S // PACK]),
-        )
+        for places in halves:
+            nc.vector.tensor_copy(
+                x_planes[:, :, places].bitcast(I32),
+                picked_scales[:, places].bitcast(I32).unsqueeze(1).to_broadcast([P, PASSES, HALF // PACK]),
+            )
         x_plane = [x_planes[:, z, :] for z in range(PASSES)]
 
         def move_odd_rows(z):
@@ -113,9 +117,9 @@ def tile_picked_phmlp_relu_p_kernel(
                 early, late = [raw[:].rearrange("p j (m t) -> p m t j", t=PACK) for raw in w1_raw1]
                 nc.scalar.activation(rounded[:, :M_EARLY, :, :PAIR], early[:, :M_EARLY], COPY)
                 nc.vector.tensor_copy(rounded[:, M_EARLY:, :, :PAIR], early[:, M_EARLY:])
-                nc.scalar.activation(rounded[:, M_LATE:, :, PAIR:], late[:, M_LATE:], COPY)
-                for m in (slice(0, LEAD), slice(LEAD, M_LATE)):
-                    nc.vector.tensor_copy(rounded[:, m, :, PAIR:], late[:, m])
+                nc.vector.tensor_copy(rounded[:, :, :PAIR, PAIR:], late[:, :, :PAIR])
+                nc.scalar.activation(rounded[:, M_LATE:, PAIR:, PAIR:], late[:, M_LATE:, PAIR:], COPY)
+                nc.vector.tensor_copy(rounded[:, :M_LATE, PAIR:, PAIR:], late[:, :M_LATE, PAIR:])
                 for cols in (slice(0, LEAD), slice(LEAD, P), slice(P, 2 * P), slice(2 * P, H)):
                     quantise(cols)
             quantised.append((w1_codes, w1_plane))

from contextlib import ExitStack

import concourse.mybir as mybir

K, T, S, H, N = 1024, 2048, 512, 512, 128
FLOPS = 2 * K * H * S + 2 * H * N * S

F32 = mybir.dt.float32
BF16 = mybir.dt.bfloat16
I32 = mybir.dt.int32
U32 = mybir.dt.uint32
U16 = mybir.dt.uint16
U8 = mybir.dt.uint8
FP8X4 = mybir.dt.float8_e4m3fn_x4
COPY = mybir.ActivationFunctionType.Copy
RELU = mybir.ActivationFunctionType.Relu

P = 128
PACK = 4
PAIR = PACK // 2
K_PASS = P * PACK
PASSES = K // K_PASS
QUADRANT = 32
GROUP = 16
HALF = S // 2
QUARTER = S // 4
PLANE_STEP = 8
M_VECTOR = 80
FIRST = 576
M_EARLY = 96
M_LATE = 40
LEAD = 64
WARM_UPS = 3
WARM_WIDTH = 32


def tile_picked_phmlp_relu_p_kernel(
    tc, x_words, x_scales, w1, w2_words, w2_scales, offs, out
):
    nc = tc.nc
    with ExitStack() as ctx:
        keep = ctx.enter_context(tc.tile_pool(name="keep", bufs=1))
        held = ctx.enter_context(tc.tile_pool(name="held", bufs=1))
        psum = ctx.enter_context(tc.psum_pool(name="psum", bufs=1))

        def w1_rows(z):
            return w1[z * K_PASS : (z + 1) * K_PASS, :].rearrange("(p j) c -> p j c", j=PACK)

        def word_rows(z):
            return x_words[z].rearrange("p c j -> p (c j)").bitcast(I32)

        offsets = keep.tile([P, S // GROUP], U16, name="offsets")

        scale_table = keep.tile([P, T], U8, name="scale_table", align_bytes=256)
        nc.vector.memset(scale_table[:].bitcast(I32), 0)
        scale_rows = x_scales.bitcast(I32).rearrange("z (g e) c -> e g z c", e=2)
        w1_raw0 = keep.tile([P, PACK, H], F32, name="w1_raw0", align_bytes=256)
        w1_raw1 = [keep.tile([P, PAIR, H], F32, name="w1_raw1a", align_bytes=256)]
        word_table = [keep.tile([P, T], I32, name="word_table0", align_bytes=256)]
        nc.sync.dma_start(word_table[0][:, :FIRST], word_rows(0)[:, :FIRST])
        nc.sync.dma_start(offsets[:], offs)
        for e in range(2):
            nc.sync.dma_start(scale_table[e:P:PLANE_STEP, :].bitcast(I32), scale_rows[e])
        nc.sync.dma_start(w1_raw0[:], w1_rows(0))
        nc.sync.dma_start(word_table[0][:, FIRST:], word_rows(0)[:, FIRST:])
        nc.sync.dma_start(w1_raw1[0][:], w1_rows(1)[:, :PAIR])

        picked_scales = held.tile([P, S], U8, name="picked_scales", align_bytes=256, offset=PAIR * H * 4 - S // 2)
        halves = [slice(half * HALF, (half + 1) * HALF) for half in range(S // HALF)]
        for places in halves:
            entries = offsets[:, places.start // GROUP : places.stop // GROUP]
            nc.vector.tensor_copy(picked_scales[:, places], scale_table[:].indirect(entries))
        x_planes = keep.tile([P, PASSES, S], U8, name="x_planes", align_bytes=64)
        for places in halves:
            nc.vector.tensor_copy(
                x_planes[:, :, places].bitcast(I32),
                picked_scales[:, places].bitcast(I32).unsqueeze(1).to_broadcast([P, PASSES, HALF // PACK]),
            )
        x_plane = [x_planes[:, z, :] for z in range(PASSES)]

        def move_odd_rows(z):
            for e in range(2):
                row = PLANE_STEP * z + e
                nc.sync.dma_start(
                    x_plane[z][row + 2 : P : QUADRANT, :].bitcast(I32),
                    x_plane[z][row + GROUP : P : QUADRANT, :].bitcast(I32),
                )

        move_odd_rows(0)
        w1_raw1.append(held.tile([P, PAIR, H], F32, name="w1_raw1b", align_bytes=256, offset=0))
        nc.sync.dma_start(w1_raw1[1][:], w1_rows(1)[:, PAIR:])
        word_table.append(held.tile([P, T], I32, name="word_table1", align_bytes=256, offset=PAIR * H * 4))
        nc.sync.dma_start(word_table[1][:], word_rows(1))
        move_odd_rows(1)

        hidden = [psum.tile([P, PACK, QUARTER], F32, name=f"hidden{u}") for u in range(S // QUARTER)]
        quantised = []
        for z in range(PASSES):
            grouped = keep.tile([P, PACK, P, PACK], BF16, name=f"w1_grouped{z}", align_bytes=64)
            rounded = grouped[:].rearrange("p t m j -> p m t j")
            w1_codes = keep.tile([P, H], U32, name=f"w1_codes{z}", align_bytes=64)
            w1_plane = keep.tile([P, H], U8, name=f"w1_plane{z}", align_bytes=64)

            def quantise(cols):
                nc.vector.quantize_mx(
                    out=w1_codes[:, cols].bitcast(FP8X4),
                    scales=w1_plane[:, cols],
                    in_=grouped[:].rearrange("p t m j -> p (t m j)")[:, PACK * cols.start : PACK * cols.stop],
                )

            if z == 0:
                exact = w1_raw0[:].rearrange("p j (m t) -> p m t j", t=PACK)
                nc.vector.tensor_copy(rounded[:, :M_VECTOR], exact[:, :M_VECTOR])
                nc.scalar.activation(rounded[:, M_VECTOR:], exact[:, M_VECTOR:], COPY)
                quantise(slice(0, H))
            else:
                early, late = [raw[:].rearrange("p j (m t) -> p m t j", t=PACK) for raw in w1_raw1]
                nc.scalar.activation(rounded[:, :M_EARLY, :, :PAIR], early[:, :M_EARLY], COPY)
                nc.vector.tensor_copy(rounded[:, M_EARLY:, :, :PAIR], early[:, M_EARLY:])
                nc.vector.tensor_copy(rounded[:, :, :PAIR, PAIR:], late[:, :, :PAIR])
                nc.scalar.activation(rounded[:, M_LATE:, PAIR:, PAIR:], late[:, M_LATE:, PAIR:], COPY)
                nc.vector.tensor_copy(rounded[:, :M_LATE, PAIR:, PAIR:], late[:, :M_LATE, PAIR:])
                for cols in (slice(0, LEAD), slice(LEAD, P), slice(P, 2 * P), slice(2 * P, H)):
                    quantise(cols)
            quantised.append((w1_codes, w1_plane))

            if z == PASSES - 1:
                unread = psum.tile([P, H], F32, name="unread", tag="acc0")
                for warm_up in range(WARM_UPS):
                    nc.tensor.matmul_mx(
                        out=unread[:WARM_WIDTH],
                        lhsT=w1_codes[:, :WARM_WIDTH].bitcast(FP8X4),
                        lhsT_scale=w1_plane[:, :WARM_WIDTH],
                        rhs=quantised[0][0][:].bitcast(FP8X4),
                        rhs_scale=quantised[0][1][:],
                        start=True,
                        stop=True,
                    )

            for half in range(S // HALF):
                tag = "w1_grouped0" if (z, half) == (0, 1) else f"picked{z}_{half}"
                picked = keep.tile([P, HALF], U32, name=f"picked{z}_{half}", tag=tag, align_bytes=64)
                entries = offsets[:, half * HALF // GROUP : (half + 1) * HALF // GROUP]
                nc.vector.tensor_copy(picked[:], word_table[z][:].bitcast(U32).indirect(entries))
                for v in range(HALF // QUARTER):
                    u = half * HALF // QUARTER + v
                    for t in range(PACK):
                        nc.tensor.matmul_mx(
                            out=hidden[u][:, t, :],
                            lhsT=w1_codes[:, t * P : (t + 1) * P].bitcast(FP8X4),
                            lhsT_scale=w1_plane[:, t * P : (t + 1) * P],
                            rhs=picked[:, v * QUARTER : (v + 1) * QUARTER].bitcast(FP8X4),
                            rhs_scale=x_plane[z][PLANE_STEP * z :, u * QUARTER : (u + 1) * QUARTER],
                            start=(z == 0 and t == 0),
                            stop=(z == PASSES - 1 and t == PACK - 1),
                        )

        w2_codes = keep.tile([P, N], I32, name="w2_codes", tag="word_table0", align_bytes=256)
        nc.sync.dma_start(w2_codes[:], w2_words[0].rearrange("p c j -> p (c j)").bitcast(I32))
        w2_plane = keep.tile([P, N], U8, name="w2_plane", tag="w1_raw0", align_bytes=256)
        nc.vector.memset(w2_plane[:].bitcast(I32), 0)
        for q in range(P // QUADRANT):
            nc.sync.dma_start(
                w2_plane[QUADRANT * q : QUADRANT * q + 4, :].bitcast(I32),
                w2_scales[0, 4 * q : 4 * q + 4, :].bitcast(I32),
            )

        banks = range(S // QUARTER)
        h = [keep.tile([P, QUARTER, PACK], BF16, name=f"h{u}", align_bytes=64) for u in banks]
        result = [keep.tile([N, QUARTER], F32, name=f"result{u}") for u in banks]
        sums = {}

        def activate(engine, u, cols):
            source = hidden[u][:, :, cols].rearrange("p t n -> p n t")
            if engine is nc.vector:
                nc.vector.tensor_scalar_max(h[u][:, cols, :], source, 0.0)
            else:
                nc.scalar.activation(h[u][:, cols, :], source, RELU)

        def multiply(u, cols, tag):
            width = cols.stop - cols.start
            h_codes = keep.tile([P, width], U32, name=f"h_codes{u}_{cols.start}", align_bytes=64)
            h_plane = keep.tile([P, width], U8, name=f"h_plane{u}_{cols.start}", align_bytes=64)
            nc.vector.quantize_mx(
                out=h_codes[:].bitcast(FP8X4), scales=h_plane[:], in_=h[u][:, cols, :].rearrange("p n t -> p (n t)")
            )
            acc = psum.tile([N, width], F32, name=f"acc{u}_{cols.start}", tag=tag)
            nc.tensor.matmul_mx(
                out=acc[:],
                lhsT=w2_codes[:].bitcast(FP8X4),
                lhsT_scale=w2_plane[:],
                rhs=h_codes[:].bitcast(FP8X4),
                rhs_scale=h_plane[:],
                start=True,
                stop=True,
            )
            sums[u, cols.start] = acc

        def copy_out(engine, u, cols):
            copy = nc.vector.tensor_copy if engine is nc.vector else nc.scalar.copy
            copy(result[u][:, cols], sums[u, cols.start][:])
            if cols.stop == QUARTER:
                nc.sync.dma_start(out[:, u * QUARTER : (u + 1) * QUARTER], result[u][:])

        whole, low, high = slice(0, QUARTER), slice(0, QUARTER // 2), slice(QUARTER // 2, QUARTER)
        activate(nc.scalar, 0, whole)
        activate(nc.vector, 1, whole)
        activate(nc.scalar, 2, whole)
        activate(nc.scalar, 3, low)
        activate(nc.scalar, 3, high)
        multiply(0, whole, "acc0")
        multiply(1, whole, "acc1")
        multiply(2, whole, "acc2")
        multiply(3, low, "acc3")
        multiply(3, high, "hidden0")
        copy_out(nc.scalar, 0, whole)
        copy_out(nc.scalar, 1, whole)
        copy_out(nc.scalar, 2, whole)
        copy_out(nc.vector, 3, low)
        copy_out(nc.vector, 3, high)
